import numpy as np
import ml_dtypes


def mxq(x, axis, fmt="e4m3"):
    dtype, down = {"e4m3": (ml_dtypes.float8_e4m3fn, 7), "e5m2": (ml_dtypes.float8_e5m2, 14)}[fmt]
    v = np.moveaxis(np.asarray(x, np.float32).astype(ml_dtypes.bfloat16).astype(np.float64), axis, -1)
    blocks = v.reshape(v.shape[:-1] + (-1, 32))
    amax = np.abs(blocks).max(-1, keepdims=True)
    byte = np.maximum(np.where(amax > 0, np.frexp(amax)[1] - 1 + 127, 0) - down, 1)
    scale = np.exp2(byte - 127.0)
    codes = (blocks / scale).astype(np.float32).astype(dtype).astype(np.float64)
    return np.moveaxis((codes * scale).reshape(v.shape), -1, axis)


WIDE = False


def mx_kscale(k):
    if not WIDE:
        return np.ones(k)
    levels = np.array([10, -10, 5, -5, 0])
    if k % 512:
        return np.exp2(np.random.permutation(np.resize(levels, k // 32))).repeat(32)
    a = np.empty((k // 512, 16))
    for p in range(k // 512):
        a[p, :8] = np.random.permutation(np.resize(levels, 8))
        for g in range(8):
            far = levels[np.abs(levels - a[p, g]) >= 10]
            a[p, g + 8] = far[np.random.randint(len(far))]
    return np.exp2(a.ravel()).repeat(32)


def f64(x):
    return np.asarray(x).astype(np.float64)


def striped(idx):
    return np.tile(idx.reshape(-1, 16).T, (8, 1)).astype(np.uint16)


def unstriped(offs):
    return offs[:16].T.reshape(-1).astype(np.int64)


E2M1 = np.array([0.0, 0.5, 1.0, 1.5, 2.0, 3.0, 4.0, 6.0, -0.0, -0.5, -1.0, -1.5, -2.0, -3.0, -4.0, -6.0])


def pack_weight(w, fmt):
    k, n = w.shape
    w = f64(np.asarray(w, np.float32).astype(ml_dtypes.bfloat16)).reshape(k // 32, 32, n)
    amax = np.abs(w).max(1)
    if fmt == "e4m3":
        byte = np.frexp(amax)[1] - 1 + 127 - 7
    else:
        mant, ex = np.frexp(amax / 6.0)
        byte = np.where(mant > 0.5, ex, ex - 1) + 127
    byte = np.clip(np.where(amax > 0, byte, 1), 1, 254)
    scaled = (w * np.exp2(127.0 - byte)[:, None, :]).reshape(k, n).astype(np.float32)
    by_word = np.ascontiguousarray(scaled.reshape(k // 512, 128, 4, n).transpose(0, 1, 3, 2))
    if fmt == "e4m3":
        words = by_word.astype(ml_dtypes.float8_e4m3fn).view(np.uint8)
    else:
        c = by_word.astype(ml_dtypes.float4_e2m1fn).view(np.uint8) & 0xF
        words = (c[..., 0::2] | (c[..., 1::2] << 4)).reshape(k // 512, 128, 2 * n)
    return np.ascontiguousarray(words), np.ascontiguousarray(byte.astype(np.uint8).reshape(k // 512, 16, n))


def unpack_weight(words, scales, fmt):
    g, _, n = scales.shape
    words = np.ascontiguousarray(words).reshape(g, 128, n, -1)
    if fmt == "e4m3":
        vals = words.view(ml_dtypes.float8_e4m3fn).astype(np.float64)
    else:
        nib = np.empty((g, 128, n, 4), np.uint8)
        nib[..., 0::2] = words & 0xF
        nib[..., 1::2] = words >> 4
        vals = E2M1[nib]
    vals = vals * np.repeat(np.exp2(scales.astype(np.float64) - 127.0), 8, axis=1)[..., None]
    return vals.transpose(0, 1, 3, 2).reshape(g * 512, n)


def relu(v):
    return np.maximum(v, 0.0)


K, T, E, N = 1024, 1280, 8, 256
COUNTS = (128, 128, 128, 640, 128, 640, 256, 512)
STARTS = np.cumsum((0,) + COUNTS)
K8 = 512


def by_expert(wq, xq):
    return np.concatenate([wq[e].T @ xq[:, STARTS[e]:STARTS[e + 1]] for e in range(E)], axis=1)


def setup_inputs():
    n = np.random.standard_normal
    s = mx_kscale(K)[:, None]
    both = np.repeat(np.arange(E), COUNTS)
    pair = np.stack([both[:T], both[T:]])[:, np.random.permutation(T)]
    pair = np.where(np.random.rand(T) < 0.5, pair, pair[::-1])
    order = np.argsort(pair.reshape(-1), kind="stable")
    slot_token = order % T; pos = np.empty(2 * T, np.int64); pos[order] = np.arange(2 * T); pos = pos.reshape(2, T)
    g = np.random.uniform(0.2, 0.8, T)
    w = n((E, K, N)) / np.sqrt(K) / s[None]
    w8 = [pack_weight(m[:K8], "e4m3") for m in w]
    w4 = [pack_weight(m[K8:], "e2m1") for m in w]
    return {
        "xT": (n((K, T)) * s).astype(np.float32),
        "w8_words": np.stack([m[0] for m in w8]),
        "w8_scales": np.stack([m[1] for m in w8]),
        "w4_words": np.stack([m[0] for m in w4]),
        "w4_scales": np.stack([m[1] for m in w4]),
        "b": (0.3 * n((N, E))).astype(np.float32),
        "gate": np.stack([np.tile(g, (N, 1)), np.tile(1.0 - g, (N, 1))]).astype(np.float32),
        "offs": striped(slot_token),
        "pos1": striped(pos[0]),
        "pos2": striped(pos[1]),
    }


def reference(xT, w8_words, w8_scales, w4_words, w4_scales, b, gate, offs, pos1, pos2):
    idx = unstriped(offs)
    w = np.stack([np.concatenate([unpack_weight(w8_words[e], w8_scales[e], "e4m3"), unpack_weight(w4_words[e], w4_scales[e], "e2m1")]) for e in range(E)])
    xq = mxq(f64(xT)[:, idx], 0, "e4m3")
    y = by_expert(w, xq)
    y = relu(y + np.repeat(f64(b), COUNTS, axis=1))
    return f64(gate[0]) * y[:, unstriped(pos1)] + f64(gate[1]) * y[:, unstriped(pos2)]

@@ -1,0 +1,157 @@
+from contextlib import ExitStack
+
+import concourse.mybir as mybir
+
+F32 = mybir.dt.float32
+BF16 = mybir.dt.bfloat16
+I32 = mybir.dt.int32
+U32 = mybir.dt.uint32
+U16 = mybir.dt.uint16
+U8 = mybir.dt.uint8
+FP8X4 = mybir.dt.float8_e4m3fn_x4
+FP4X4 = mybir.dt.float4_e2m1fn_x4
+COPY = mybir.ActivationFunctionType.Copy
+RELU = mybir.ActivationFunctionType.Relu
+MULT = mybir.AluOpType.mult
+ADD = mybir.AluOpType.add
+MAX = mybir.AluOpType.max
+
+P = 128
+K, T, E, N = 1024, 1280, 8, 256
+COUNTS = (128, 128, 128, 640, 128, 640, 256, 512)
+SLOTS = sum(COUNTS)
+STARTS = tuple(sum(COUNTS[:e]) for e in range(E))
+HALVES = N // P
+
+FLOPS = 2 * SLOTS * K * N
+BYTES = 4 * K * T + (4 + 2) * 128 * E * N + 2 * 16 * E * N + 4 * N * E + 4 * 2 * T + 2 * 128 * (160 + 80 + 80) + 4 * N * T
+
+CHUNKS = ((0, 512), (512, 1024), (1024, 1280))
+VECTOR_SHARE = ((320, 320, 160), (0, 0, 128))
+WORD0_PIECES = ((0, 896), (896, 1728), (1728, 2560))
+PIECES = ((0, 384, (0, 1, 2)), (384, 1024, (3,)), (1024, 1792, (4, 5)), (2048, 2560, (7,)), (1792, 2048, (6,)))
+COMBINE = (((0, 1280),), ((0, 640), (640, 1024), (1024, 1280)))
+
+
+def tile_moe_rag_lin_relu_kernel(tc, xT, w8_words, w8_scales, w4_words, w4_scales, b, gate, offs, pos1, pos2, out):
+    nc = tc.nc
+    with ExitStack() as ctx:
+        keep = ctx.enter_context(tc.tile_pool(name="keep", bufs=1))
+        psum = ctx.enter_context(tc.psum_pool(name="psum", bufs=8))
+
+        offs_sb = keep.tile([P, SLOTS // 16], U16, name="offs_sb")
+        pos1_sb = keep.tile([P, T // 16], U16, name="pos1_sb")
+        pos2_sb = keep.tile([P, T // 16], U16, name="pos2_sb")
+
+        codes = [keep.tile([P, T], U32, name=f"codes{a}", align_bytes=64) for a in range(2)]
+        scales = keep.tile([P, T], U8, name="scales", align_bytes=64)
+        slot_codes = [keep.tile([P, SLOTS], U32, name=f"slot_codes{a}", align_bytes=64) for a in range(2)]
+        slot_scales = keep.tile([P, SLOTS], U8, name="slot_scales", align_bytes=64)
+        w8_sb = keep.tile([P, E, 4 * N], U8, name="w8_sb", align_bytes=64)
+        w4_sb = keep.tile([P, E, 2 * N], U8, name="w4_sb", align_bytes=64)
+        w_scales = keep.tile([P, E, N], U8, name="w_scales", align_bytes=64)
+        b_sb = keep.tile([P, HALVES, E], F32, name="b_sb")
+        gates = [keep.tile([P, T], F32, name=f"gate{i}") for i in range(2)]
+        y = [keep.tile([P, SLOTS], F32, name=f"y{h}") for h in range(HALVES)]
+
+        nc.gpsimd.memset(scales[:], 0)
+        nc.gpsimd.memset(w_scales[:].bitcast(I32), 0)
+
+        raw = {}
+        for a in range(2):
+            rows = xT[512 * a : 512 * (a + 1), :].rearrange("(p j) t -> p j t", j=4)
+            for c, (c0, c1) in enumerate(CHUNKS):
+                raw[a, c] = keep.tile([P, 4, c1 - c0], F32, name=f"raw{a}_{c}")
+                nc.sync.dma_start(out=raw[a, c][:], in_=rows[:, :, c0:c1])
+            if a == 0:
+                nc.sync.dma_start(offs_sb[:], offs)
+        for src, row in ((w4_scales, 0), (w8_scales, 4)):
+            for q in range(4):
+                nc.sync.dma_start(
+                    out=w_scales[32 * q + row : 32 * q + row + 4, :, :].bitcast(I32),
+                    in_=src.rearrange("e a q n -> q (e a) n")[4 * q : 4 * q + 4].bitcast(I32),
+                )
+        w8_view = w8_words.rearrange("e a p n r -> p (e a) (n r)")
+        w4_view = w4_words.rearrange("e a p m -> p (e a) m")
+        nc.sync.dma_start(out=b_sb[:], in_=b.rearrange("(h p) e -> p h e", h=HALVES))
+        for e0 in (0, 4):
+            nc.sync.dma_start(out=w8_sb[:, e0 : e0 + 4, :].bitcast(I32), in_=w8_view[:, e0 : e0 + 4, :].bitcast(I32))
+            nc.sync.dma_start(out=w4_sb[:, e0 : e0 + 4, :].bitcast(I32), in_=w4_view[:, e0 : e0 + 4, :].bitcast(I32))
+        nc.sync.dma_start(pos1_sb[:], pos1)
+        nc.sync.dma_start(pos2_sb[:], pos2)
+        for i in range(2):
+            nc.sync.dma_start(out=gates[i][:], in_=gate[i, 0:P, :])
+
+        def cast_and_quantize(a):
+            grouped = []
+            for c, (c0, c1) in enumerate(CHUNKS):
+                g = keep.tile([P, c1 - c0, 4], BF16, name=f"grouped{a}_{c}", align_bytes=64)
+                grouped.append(g)
+                v = VECTOR_SHARE[a][c]
+                if v:
+                    nc.vector.tensor_copy(out=g[:, :v, :], in_=raw[a, c][:, :, :v].rearrange("p j t -> p t j"))
+                if v < c1 - c0:
+                    nc.scalar.activation(g[:, v:, :], raw[a, c][:, :, v:].rearrange("p j t -> p t j"), COPY)
+            for c, (c0, c1) in enumerate(CHUNKS):
+                nc.vector.quantize_mx(
+                    out=codes[a][:, c0:c1].bitcast(FP8X4),
+                    scales=scales[4 * (1 - a) :, c0:c1],
+                    in_=grouped[c][:].rearrange("p t j -> p (t j)"),
+                )
+
+        def take(window, result, s0, s1):
+            nc.vector.tensor_copy(result[:, s0:s1], window[:].indirect(offs_sb[:, s0 // 16 : s1 // 16]))
+
+        cast_and_quantize(0)
+        for s0, s1 in WORD0_PIECES:
+            take(codes[0], slot_codes[0], s0, s1)
+        cast_and_quantize(1)
+
+        for s0, s1, experts in PIECES:
+            take(codes[1], slot_codes[1], s0, s1)
+            take(scales, slot_scales, s0, s1)
+            for h in range(HALVES):
+                for e in experts:
+                    done = 0
+                    while done < COUNTS[e]:
+                        width = min(128 if (e == 6 and h == 0) else 512, COUNTS[e] - done)
+                        step = 512 if width == 512 else 128
+                        acc = psum.tile([P, 512], F32, name="acc")
+                        for g0 in range(0, width, step):
+                            j0 = STARTS[e] + done + g0
+                            j1 = j0 + step
+                            nc.tensor.matmul_mx(
+                                out=acc[:, g0 : g0 + step],
+                                lhsT=w8_sb[:, e, 512 * h : 512 * (h + 1)].bitcast(FP8X4),
+                                lhsT_scale=w_scales[4:, e, P * h : P * (h + 1)],
+                                rhs=slot_codes[0][:, j0:j1].bitcast(FP8X4),
+                                rhs_scale=slot_scales[4:, j0:j1],
+                                start=True,
+                                stop=False,
+                            )
+                            nc.tensor.matmul_mx(
+                                out=acc[:, g0 : g0 + step],
+                                lhsT=w4_sb[:, e, 256 * h : 256 * (h + 1)].bitcast(FP4X4),
+                                lhsT_scale=w_scales[:, e, P * h : P * (h + 1)],
+                                rhs=slot_codes[1][:, j0:j1].bitcast(FP8X4),
+                                rhs_scale=slot_scales[:, j0:j1],
+                                start=False,
+                                stop=True,
+                            )
+                        j0 = STARTS[e] + done
+                        if e == 6 and h == 0 and done:
+                            nc.vector.tensor_scalar(y[h][:, j0 : j0 + width], acc[:, :width], b_sb[:, h, e : e + 1], 0.0, op0=ADD, op1=MAX)
+                        else:
+                            nc.scalar.activation(y[h][:, j0 : j0 + width], acc[:, :width], RELU, bias=b_sb[:, h, e : e + 1])
+                        done += width
+
+        for h in range(HALVES):
+            for t0, t1 in COMBINE[h]:
+                first = keep.tile([P, t1 - t0], F32, name=f"first{h}_{t0}")
+                second = keep.tile([P, t1 - t0], F32, name=f"second{h}_{t0}")
+                total = keep.tile([P, t1 - t0], F32, name=f"total{h}_{t0}")
+                cols = slice(t0 // 16, t1 // 16)
+                nc.vector.tensor_tensor(first[:], y[h][:].indirect(pos1_sb[:, cols]), gates[0][:, t0:t1], MULT)
+                nc.vector.tensor_tensor(second[:], y[h][:].indirect(pos2_sb[:, cols]), gates[1][:, t0:t1], MULT)
+                nc.vector.tensor_tensor(total[:], first[:], second[:], ADD)
+                nc.sync.dma_start(out=out[P * h : P * (h + 1), t0:t1], in_=total[:])

@@ -27,10 +27,15 @@ FLOPS = 2 * SLOTS * K * N
 BYTES = 4 * K * T + (4 + 2) * 128 * E * N + 2 * 16 * E * N + 4 * N * E + 4 * 2 * T + 2 * 128 * (160 + 80 + 80) + 4 * N * T
 
 CHUNKS = ((0, 512), (512, 1024), (1024, 1280))
-VECTOR_SHARE = ((320, 320, 160), (0, 0, 128))
+VECTOR_SHARE = ((320, 320, 192), (0, 0, 128))
 WORD0_PIECES = ((0, 896), (896, 1728), (1728, 2560))
-PIECES = ((0, 384, (0, 1, 2)), (384, 1024, (3,)), (1024, 1792, (4, 5)), (2048, 2560, (7,)), (1792, 2048, (6,)))
-COMBINE = (((0, 1280),), ((0, 640), (640, 1024), (1024, 1280)))
+PIECES = (
+    (0, 896, ((0, 0, 128), (1, 128, 256), (2, 256, 384), (3, 384, 896))),
+    (896, 1792, ((3, 896, 1024), (4, 1024, 1152), (5, 1152, 1664), (5, 1664, 1792))),
+    (2048, 2560, ((7, 2048, 2560),)),
+    (1792, 2048, ((6, 1792, 1920), (6, 1920, 2048))),
+)
+COMBINE = ((0, 0, 1280), (1, 0, 640), (1, 640, 1024), (1, 1024, 1280))
 
 
 def tile_moe_rag_lin_relu_kernel(tc, xT, w8_words, w8_scales, w4_words, w4_scales, b, gate, offs, pos1, pos2, out):
@@ -82,76 +87,93 @@ def tile_moe_rag_lin_relu_kernel(tc, xT, w8_words, w8_scales, w4_words, w4_scale
         for i in range(2):
             nc.sync.dma_start(out=gates[i][:], in_=gate[i, 0:P, :])
 
-        def cast_and_quantize(a):
-            grouped = []
-            for c, (c0, c1) in enumerate(CHUNKS):
-                g = keep.tile([P, c1 - c0, 4], BF16, name=f"grouped{a}_{c}", align_bytes=64)
-                grouped.append(g)
-                v = VECTOR_SHARE[a][c]
-                if v:
-                    nc.vector.tensor_copy(out=g[:, :v, :], in_=raw[a, c][:, :, :v].rearrange("p j t -> p t j"))
-                if v < c1 - c0:
-                    nc.scalar.activation(g[:, v:, :], raw[a, c][:, :, v:].rearrange("p j t -> p t j"), COPY)
-            for c, (c0, c1) in enumerate(CHUNKS):
-                nc.vector.quantize_mx(
-                    out=codes[a][:, c0:c1].bitcast(FP8X4),
-                    scales=scales[4 * (1 - a) :, c0:c1],
-                    in_=grouped[c][:].rearrange("p t j -> p (t j)"),
-                )
+        grouped = {}
+
+        def cast(a, c):
+            c0, c1 = CHUNKS[c]
+            g = keep.tile([P, c1 - c0, 4], BF16, name=f"grouped{a}_{c}", align_bytes=64)
+            grouped[a, c] = g
+            dst = g[:].rearrange("p (t i) j -> p t j i", i=4)
+            src = raw[a, c][:].rearrange("p j (t i) -> p t j i", i=4)
+            v = VECTOR_SHARE[a][c] // 4
+            if v:
+                nc.vector.tensor_copy(out=dst[:, :v], in_=src[:, :v])
+            if 4 * v < c1 - c0:
+                nc.scalar.activation(dst[:, v:], src[:, v:], COPY)
+
+        def quantize(a, c):
+            c0, c1 = CHUNKS[c]
+            nc.vector.quantize_mx(
+                out=codes[a][:, c0:c1].bitcast(FP8X4),
+                scales=scales[4 * (1 - a) :, c0:c1],
+                in_=grouped[a, c][:].rearrange("p t j -> p (t j)"),
+            )
 
         def take(window, result, s0, s1):
             nc.vector.tensor_copy(result[:, s0:s1], window[:].indirect(offs_sb[:, s0 // 16 : s1 // 16]))
 
-        cast_and_quantize(0)
-        for s0, s1 in WORD0_PIECES:
-            take(codes[0], slot_codes[0], s0, s1)
-        cast_and_quantize(1)
+        cast(0, 0)
+        cast(0, 1)
+        quantize(0, 0)
+        cast(0, 2)
+        quantize(0, 1)
+        quantize(0, 2)
+        take(codes[0], slot_codes[0], *WORD0_PIECES[0])
+        take(codes[0], slot_codes[0], *WORD0_PIECES[1])
+        take(codes[0], slot_codes[0], *WORD0_PIECES[2])
+        cast(1, 0)
+        cast(1, 1)
+        cast(1, 2)
+        quantize(1, 0)
+        quantize(1, 1)
+        quantize(1, 2)
 
-        for s0, s1, experts in PIECES:
+        for s0, s1, banks in PIECES:
             take(codes[1], slot_codes[1], s0, s1)
             take(scales, slot_scales, s0, s1)
             for h in range(HALVES):
-                for e in experts:
-                    done = 0
-                    while done < COUNTS[e]:
-                        width = min(128 if (e == 6 and h == 0) else 512, COUNTS[e] - done)
-                        step = 512 if width == 512 else 128
-                        acc = psum.tile([P, 512], F32, name="acc")
-                        for g0 in range(0, width, step):
-                            j0 = STARTS[e] + done + g0
-                            j1 = j0 + step
-                            nc.tensor.matmul_mx(
-                                out=acc[:, g0 : g0 + step],
-                                lhsT=w8_sb[:, e, 512 * h : 512 * (h + 1)].bitcast(FP8X4),
-                                lhsT_scale=w_scales[4:, e, P * h : P * (h + 1)],
-                                rhs=slot_codes[0][:, j0:j1].bitcast(FP8X4),
-                                rhs_scale=slot_scales[4:, j0:j1],
-                                start=True,
-                                stop=False,
-                            )
-                            nc.tensor.matmul_mx(
-                                out=acc[:, g0 : g0 + step],
-                                lhsT=w4_sb[:, e, 256 * h : 256 * (h + 1)].bitcast(FP4X4),
-                                lhsT_scale=w_scales[:, e, P * h : P * (h + 1)],
-                                rhs=slot_codes[1][:, j0:j1].bitcast(FP8X4),
-                                rhs_scale=slot_scales[:, j0:j1],
-                                start=False,
-                                stop=True,
-                            )
-                        j0 = STARTS[e] + done
-                        if e == 6 and h == 0 and done:
-                            nc.vector.tensor_scalar(y[h][:, j0 : j0 + width], acc[:, :width], b_sb[:, h, e : e + 1], 0.0, op0=ADD, op1=MAX)
-                        else:
-                            nc.scalar.activation(y[h][:, j0 : j0 + width], acc[:, :width], RELU, bias=b_sb[:, h, e : e + 1])
-                        done += width
+                for e, b0, b1 in banks:
+                    acc = psum.tile([P, b1 - b0], F32, name="acc")
+                    nc.tensor.matmul_mx(
+                        out=acc[:],
+                        lhsT=w8_sb[:, e, 512 * h : 512 * (h + 1)].bitcast(FP8X4),
+                        lhsT_scale=w_scales[4:, e, P * h : P * (h + 1)],
+                        rhs=slot_codes[0][:, b0:b1].bitcast(FP8X4),
+                        rhs_scale=slot_scales[4:, b0:b1],
+                        start=True,
+                        stop=False,
+                    )
+                    nc.tensor.matmul_mx(
+                        out=acc[:],
+                        lhsT=w4_sb[:, e, 256 * h : 256 * (h + 1)].bitcast(FP4X4),
+                        lhsT_scale=w_scales[:, e, P * h : P * (h + 1)],
+                        rhs=slot_codes[1][:, b0:b1].bitcast(FP8X4),
+                        rhs_scale=slot_scales[:, b0:b1],
+                        start=False,
+                        stop=True,
+                    )
+                    if h == 0 and b0 == 1920:
+                        nc.vector.tensor_scalar(y[h][:, b0:b1], acc[:], b_sb[:, h, e : e + 1], 0.0, op0=ADD, op1=MAX)
+                    else:
+                        nc.scalar.activation(y[h][:, b0:b1], acc[:], RELU, bias=b_sb[:, h, e : e + 1])
 
-        for h in range(HALVES):
-            for t0, t1 in COMBINE[h]:
-                first = keep.tile([P, t1 - t0], F32, name=f"first{h}_{t0}")
-                second = keep.tile([P, t1 - t0], F32, name=f"second{h}_{t0}")
-                total = keep.tile([P, t1 - t0], F32, name=f"total{h}_{t0}")
-                cols = slice(t0 // 16, t1 // 16)
-                nc.vector.tensor_tensor(first[:], y[h][:].indirect(pos1_sb[:, cols]), gates[0][:, t0:t1], MULT)
-                nc.vector.tensor_tensor(second[:], y[h][:].indirect(pos2_sb[:, cols]), gates[1][:, t0:t1], MULT)
-                nc.vector.tensor_tensor(total[:], first[:], second[:], ADD)
-                nc.sync.dma_start(out=out[P * h : P * (h + 1), t0:t1], in_=total[:])
+        def product(c, i):
+            h, t0, t1 = COMBINE[c]
+            result = keep.tile([P, t1 - t0], F32, name=f"product{c}_{i}")
+            pos = (pos1_sb, pos2_sb)[i]
+            nc.vector.tensor_tensor(result[:], y[h][:].indirect(pos[:, t0 // 16 : t1 // 16]), gates[i][:, t0:t1], MULT)
+            return result
+
+        def add_and_store(c, first, second):
+            h, t0, t1 = COMBINE[c]
+            total = keep.tile([P, t1 - t0], F32, name=f"total{c}")
+            nc.vector.tensor_tensor(total[:], first[:], second[:], ADD)
+            nc.sync.dma_start(out=out[P * h : P * (h + 1), t0:t1], in_=total[:])
+
+        held = None
+        for c in range(len(COMBINE)):
+            first = product(c, 0)
+            if held:
+                add_and_store(c - 1, *held)
+            held = (first, product(c, 1))
+        add_and_store(len(COMBINE) - 1, *held)

@@ -27,15 +27,15 @@ FLOPS = 2 * SLOTS * K * N
 BYTES = 4 * K * T + (4 + 2) * 128 * E * N + 2 * 16 * E * N + 4 * N * E + 4 * 2 * T + 2 * 128 * (160 + 80 + 80) + 4 * N * T
 
 CHUNKS = ((0, 512), (512, 1024), (1024, 1280))
-VECTOR_SHARE = ((320, 320, 192), (0, 0, 128))
-WORD0_PIECES = ((0, 896), (896, 1728), (1728, 2560))
+VECTOR_SHARE = ((320, 320, 192), (0, 0, 192))
+WORD0_PIECES = ((0, 960), (960, 1920), (1920, 2560))
 PIECES = (
     (0, 896, ((0, 0, 128), (1, 128, 256), (2, 256, 384), (3, 384, 896))),
     (896, 1792, ((3, 896, 1024), (4, 1024, 1152), (5, 1152, 1664), (5, 1664, 1792))),
     (2048, 2560, ((7, 2048, 2560),)),
     (1792, 2048, ((6, 1792, 1920), (6, 1920, 2048))),
 )
-COMBINE = ((0, 0, 1280), (1, 0, 640), (1, 640, 1024), (1, 1024, 1280))
+COMBINE = ((0, 0, 1280), (1, 0, 896), (1, 896, 1280))
 
 
 def tile_moe_rag_lin_relu_kernel(tc, xT, w8_words, w8_scales, w4_words, w4_scales, b, gate, offs, pos1, pos2, out):
@@ -120,42 +120,57 @@ def tile_moe_rag_lin_relu_kernel(tc, xT, w8_words, w8_scales, w4_words, w4_scale
         quantize(0, 2)
         take(codes[0], slot_codes[0], *WORD0_PIECES[0])
         take(codes[0], slot_codes[0], *WORD0_PIECES[1])
-        take(codes[0], slot_codes[0], *WORD0_PIECES[2])
         cast(1, 0)
         cast(1, 1)
-        cast(1, 2)
         quantize(1, 0)
+        take(codes[0], slot_codes[0], *WORD0_PIECES[2])
+        cast(1, 2)
         quantize(1, 1)
         quantize(1, 2)
 
-        for s0, s1, banks in PIECES:
-            take(codes[1], slot_codes[1], s0, s1)
+        def multiply(acc, a, h, e, b0, b1):
+            nc.tensor.matmul_mx(
+                out=acc[:],
+                lhsT=(w8_sb[:, e, 512 * h : 512 * (h + 1)].bitcast(FP8X4), w4_sb[:, e, 256 * h : 256 * (h + 1)].bitcast(FP4X4))[a],
+                lhsT_scale=w_scales[4 * (1 - a) :, e, P * h : P * (h + 1)],
+                rhs=slot_codes[a][:, b0:b1].bitcast(FP8X4),
+                rhs_scale=slot_scales[4 * (1 - a) :, b0:b1],
+                start=a == 0,
+                stop=a == 1,
+            )
+
+        def empty(acc, h, e, b0, b1):
+            if h == 0 and b0 == 1920:
+                nc.vector.tensor_scalar(y[h][:, b0:b1], acc[:], b_sb[:, h, e : e + 1], 0.0, op0=ADD, op1=MAX)
+            else:
+                nc.scalar.activation(y[h][:, b0:b1], acc[:], RELU, bias=b_sb[:, h, e : e + 1])
+
+        def experts(h, banks):
+            for e, b0, b1 in banks:
+                acc = psum.tile([P, b1 - b0], F32, name="acc")
+                multiply(acc, 0, h, e, b0, b1)
+                multiply(acc, 1, h, e, b0, b1)
+                empty(acc, h, e, b0, b1)
+
+        for i, (s0, s1, banks) in enumerate(PIECES[:-1]):
             take(scales, slot_scales, s0, s1)
-            for h in range(HALVES):
-                for e, b0, b1 in banks:
-                    acc = psum.tile([P, b1 - b0], F32, name="acc")
-                    nc.tensor.matmul_mx(
-                        out=acc[:],
-                        lhsT=w8_sb[:, e, 512 * h : 512 * (h + 1)].bitcast(FP8X4),
-                        lhsT_scale=w_scales[4:, e, P * h : P * (h + 1)],
-                        rhs=slot_codes[0][:, b0:b1].bitcast(FP8X4),
-                        rhs_scale=slot_scales[4:, b0:b1],
-                        start=True,
-                        stop=False,
-                    )
-                    nc.tensor.matmul_mx(
-                        out=acc[:],
-                        lhsT=w4_sb[:, e, 256 * h : 256 * (h + 1)].bitcast(FP4X4),
-                        lhsT_scale=w_scales[:, e, P * h : P * (h + 1)],
-                        rhs=slot_codes[1][:, b0:b1].bitcast(FP8X4),
-                        rhs_scale=slot_scales[:, b0:b1],
-                        start=False,
-                        stop=True,
-                    )
-                    if h == 0 and b0 == 1920:
-                        nc.vector.tensor_scalar(y[h][:, b0:b1], acc[:], b_sb[:, h, e : e + 1], 0.0, op0=ADD, op1=MAX)
-                    else:
-                        nc.scalar.activation(y[h][:, b0:b1], acc[:], RELU, bias=b_sb[:, h, e : e + 1])
+            take(codes[1], slot_codes[1], s0, s1)
+            experts(0, banks)
+            if i < 2:
+                experts(1, banks)
+        s0, s1, banks = PIECES[-1]
+        take(scales, slot_scales, s0, s1)
+        sums = []
+        for e, b0, b1 in banks:
+            acc = psum.tile([P, b1 - b0], F32, name="acc")
+            sums.append(acc)
+            multiply(acc, 0, 0, e, b0, b1)
+        take(codes[1], slot_codes[1], s0, s1)
+        for acc, (e, b0, b1) in zip(sums, banks):
+            multiply(acc, 1, 0, e, b0, b1)
+            empty(acc, 0, e, b0, b1)
+        for s0, s1, banks in PIECES[2:]:
+            experts(1, banks)
 
         def product(c, i):
             h, t0, t1 = COMBINE[c]

@@ -70,18 +70,18 @@ def tile_moe_rag_lin_relu_kernel(tc, xT, w8_words, w8_scales, w4_words, w4_scale
                 nc.sync.dma_start(out=raw[a, c][:], in_=rows[:, :, c0:c1])
             if a == 0:
                 nc.sync.dma_start(offs_sb[:], offs)
+        w8_view = w8_words.rearrange("e a p n r -> p (e a) (n r)")
+        w4_view = w4_words.rearrange("e a p m -> p (e a) m")
+        for e0 in (0, 4):
+            nc.sync.dma_start(out=w8_sb[:, e0 : e0 + 4, :].bitcast(I32), in_=w8_view[:, e0 : e0 + 4, :].bitcast(I32))
+            nc.sync.dma_start(out=w4_sb[:, e0 : e0 + 4, :].bitcast(I32), in_=w4_view[:, e0 : e0 + 4, :].bitcast(I32))
         for src, row in ((w4_scales, 0), (w8_scales, 4)):
             for q in range(4):
                 nc.sync.dma_start(
                     out=w_scales[32 * q + row : 32 * q + row + 4, :, :].bitcast(I32),
                     in_=src.rearrange("e a q n -> q (e a) n")[4 * q : 4 * q + 4].bitcast(I32),
                 )
-        w8_view = w8_words.rearrange("e a p n r -> p (e a) (n r)")
-        w4_view = w4_words.rearrange("e a p m -> p (e a) m")
         nc.sync.dma_start(out=b_sb[:], in_=b.rearrange("(h p) e -> p h e", h=HALVES))
-        for e0 in (0, 4):
-            nc.sync.dma_start(out=w8_sb[:, e0 : e0 + 4, :].bitcast(I32), in_=w8_view[:, e0 : e0 + 4, :].bitcast(I32))
-            nc.sync.dma_start(out=w4_sb[:, e0 : e0 + 4, :].bitcast(I32), in_=w4_view[:, e0 : e0 + 4, :].bitcast(I32))
         nc.sync.dma_start(pos1_sb[:], pos1)
         nc.sync.dma_start(pos2_sb[:], pos2)
         for i in range(2):

@@ -70,18 +70,18 @@ def tile_moe_rag_lin_relu_kernel(tc, xT, w8_words, w8_scales, w4_words, w4_scale
                 nc.sync.dma_start(out=raw[a, c][:], in_=rows[:, :, c0:c1])
             if a == 0:
                 nc.sync.dma_start(offs_sb[:], offs)
-        w8_view = w8_words.rearrange("e a p n r -> p (e a) (n r)")
-        w4_view = w4_words.rearrange("e a p m -> p (e a) m")
-        for e0 in (0, 4):
-            nc.sync.dma_start(out=w8_sb[:, e0 : e0 + 4, :].bitcast(I32), in_=w8_view[:, e0 : e0 + 4, :].bitcast(I32))
-            nc.sync.dma_start(out=w4_sb[:, e0 : e0 + 4, :].bitcast(I32), in_=w4_view[:, e0 : e0 + 4, :].bitcast(I32))
         for src, row in ((w4_scales, 0), (w8_scales, 4)):
             for q in range(4):
                 nc.sync.dma_start(
                     out=w_scales[32 * q + row : 32 * q + row + 4, :, :].bitcast(I32),
                     in_=src.rearrange("e a q n -> q (e a) n")[4 * q : 4 * q + 4].bitcast(I32),
                 )
+        w8_view = w8_words.rearrange("e a p n r -> p (e a) (n r)")
+        w4_view = w4_words.rearrange("e a p m -> p (e a) m")
         nc.sync.dma_start(out=b_sb[:], in_=b.rearrange("(h p) e -> p h e", h=HALVES))
+        for e0 in (0, 4):
+            nc.sync.dma_start(out=w8_sb[:, e0 : e0 + 4, :].bitcast(I32), in_=w8_view[:, e0 : e0 + 4, :].bitcast(I32))
+            nc.sync.dma_start(out=w4_sb[:, e0 : e0 + 4, :].bitcast(I32), in_=w4_view[:, e0 : e0 + 4, :].bitcast(I32))
         nc.sync.dma_start(pos1_sb[:], pos1)
         nc.sync.dma_start(pos2_sb[:], pos2)
         for i in range(2):
@@ -153,13 +153,12 @@ def tile_moe_rag_lin_relu_kernel(tc, xT, w8_words, w8_scales, w4_words, w4_scale
                 empty(acc, h, e, b0, b1)
 
         for i, (s0, s1, banks) in enumerate(PIECES[:-1]):
-            take(scales, slot_scales, s0, s1)
+            take(scales, slot_scales, *((0, 896), (896, 1792), (1792, 2560))[i])
             take(codes[1], slot_codes[1], s0, s1)
             experts(0, banks)
-            if i < 2:
+            if i == 0:
                 experts(1, banks)
         s0, s1, banks = PIECES[-1]
-        take(scales, slot_scales, s0, s1)
         sums = []
         for e, b0, b1 in banks:
             acc = psum.tile([P, b1 - b0], F32, name="acc")
@@ -169,7 +168,7 @@ def tile_moe_rag_lin_relu_kernel(tc, xT, w8_words, w8_scales, w4_words, w4_scale
         for acc, (e, b0, b1) in zip(sums, banks):
             multiply(acc, 1, 0, e, b0, b1)
             empty(acc, 0, e, b0, b1)
-        for s0, s1, banks in PIECES[2:]:
+        for s0, s1, banks in PIECES[1:]:
             experts(1, banks)
 
         def product(c, i):

from contextlib import ExitStack

import concourse.mybir as mybir

F32 = mybir.dt.float32
BF16 = mybir.dt.bfloat16
I32 = mybir.dt.int32
U32 = mybir.dt.uint32
U16 = mybir.dt.uint16
U8 = mybir.dt.uint8
FP8X4 = mybir.dt.float8_e4m3fn_x4
FP4X4 = mybir.dt.float4_e2m1fn_x4
COPY = mybir.ActivationFunctionType.Copy
RELU = mybir.ActivationFunctionType.Relu
MULT = mybir.AluOpType.mult
ADD = mybir.AluOpType.add
MAX = mybir.AluOpType.max

P = 128
K, T, E, N = 1024, 1280, 8, 256
COUNTS = (128, 128, 128, 640, 128, 640, 256, 512)
SLOTS = sum(COUNTS)
STARTS = tuple(sum(COUNTS[:e]) for e in range(E))
HALVES = N // P

FLOPS = 2 * SLOTS * K * N
BYTES = 4 * K * T + (4 + 2) * 128 * E * N + 2 * 16 * E * N + 4 * N * E + 4 * 2 * T + 2 * 128 * (160 + 80 + 80) + 4 * N * T

CHUNKS = ((0, 512), (512, 1024), (1024, 1280))
VECTOR_SHARE = ((320, 320, 192), (0, 0, 192))
WORD0_PIECES = ((0, 960), (960, 1920), (1920, 2560))
PIECES = (
    (0, 896, ((0, 0, 128), (1, 128, 256), (2, 256, 384), (3, 384, 896))),
    (896, 1792, ((3, 896, 1024), (4, 1024, 1152), (5, 1152, 1664), (5, 1664, 1792))),
    (2048, 2560, ((7, 2048, 2560),)),
    (1792, 2048, ((6, 1792, 1920), (6, 1920, 2048))),
)
COMBINE = ((0, 0, 1280), (1, 0, 896), (1, 896, 1280))


def tile_moe_rag_lin_relu_kernel(tc, xT, w8_words, w8_scales, w4_words, w4_scales, b, gate, offs, pos1, pos2, out):
    nc = tc.nc
    with ExitStack() as ctx:
        keep = ctx.enter_context(tc.tile_pool(name="keep", bufs=1))
        psum = ctx.enter_context(tc.psum_pool(name="psum", bufs=8))

        offs_sb = keep.tile([P, SLOTS // 16], U16, name="offs_sb")
        pos1_sb = keep.tile([P, T // 16], U16, name="pos1_sb")
        pos2_sb = keep.tile([P, T // 16], U16, name="pos2_sb")

        codes = [keep.tile([P, T], U32, name=f"codes{a}", align_bytes=64) for a in range(2)]
        scales = keep.tile([P, T], U8, name="scales", align_bytes=64)
        slot_codes = [keep.tile([P, SLOTS], U32, name=f"slot_codes{a}", align_bytes=64) for a in range(2)]
        slot_scales = keep.tile([P, SLOTS], U8, name="slot_scales", align_bytes=64)
        w8_sb = keep.tile([P, E, 4 * N], U8, name="w8_sb", align_bytes=64)
        w4_sb = keep.tile([P, E, 2 * N], U8, name="w4_sb", align_bytes=64)
        w_scales = keep.tile([P, E, N], U8, name="w_scales", align_bytes=64)
        b_sb = keep.tile([P, HALVES, E], F32, name="b_sb")
        gates = [keep.tile([P, T], F32, name=f"gate{i}") for i in range(2)]
        y = [keep.tile([P, SLOTS], F32, name=f"y{h}") for h in range(HALVES)]

        nc.gpsimd.memset(scales[:], 0)
        nc.gpsimd.memset(w_scales[:].bitcast(I32), 0)

        raw = {}
        for a in range(2):
            rows = xT[512 * a : 512 * (a + 1), :].rearrange("(p j) t -> p j t", j=4)
            for c, (c0, c1) in enumerate(CHUNKS):
                raw[a, c] = keep.tile([P, 4, c1 - c0], F32, name=f"raw{a}_{c}")
                nc.sync.dma_start(out=raw[a, c][:], in_=rows[:, :, c0:c1])
            if a == 0:
                nc.sync.dma_start(offs_sb[:], offs)
        for src, row in ((w4_scales, 0), (w8_scales, 4)):
            for q in range(4):
                nc.sync.dma_start(
                    out=w_scales[32 * q + row : 32 * q + row + 4, :, :].bitcast(I32),
                    in_=src.rearrange("e a q n -> q (e a) n")[4 * q : 4 * q + 4].bitcast(I32),
                )
        w8_view = w8_words.rearrange("e a p n r -> p (e a) (n r)")
        w4_view = w4_words.rearrange("e a p m -> p (e a) m")
        nc.sync.dma_start(out=b_sb[:], in_=b.rearrange("(h p) e -> p h e", h=HALVES))
        for e0 in (0, 4):
            nc.sync.dma_start(out=w8_sb[:, e0 : e0 + 4, :].bitcast(I32), in_=w8_view[:, e0 : e0 + 4, :].bitcast(I32))
            nc.sync.dma_start(out=w4_sb[:, e0 : e0 + 4, :].bitcast(I32), in_=w4_view[:, e0 : e0 + 4, :].bitcast(I32))
        nc.sync.dma_start(pos1_sb[:], pos1)
        nc.sync.dma_start(pos2_sb[:], pos2)
        for i in range(2):
            nc.sync.dma_start(out=gates[i][:], in_=gate[i, 0:P, :])

        grouped = {}

        def cast(a, c):
            c0, c1 = CHUNKS[c]
            g = keep.tile([P, c1 - c0, 4], BF16, name=f"grouped{a}_{c}", align_bytes=64)
            grouped[a, c] = g
            dst = g[:].rearrange("p (t i) j -> p t j i", i=4)
            src = raw[a, c][:].rearrange("p j (t i) -> p t j i", i=4)
            v = VECTOR_SHARE[a][c] // 4
            if v:
                nc.vector.tensor_copy(out=dst[:, :v], in_=src[:, :v])
            if 4 * v < c1 - c0:
                nc.scalar.activation(dst[:, v:], src[:, v:], COPY)

        def quantize(a, c):
            c0, c1 = CHUNKS[c]
            nc.vector.quantize_mx(
                out=codes[a][:, c0:c1].bitcast(FP8X4),
                scales=scales[4 * (1 - a) :, c0:c1],
                in_=grouped[a, c][:].rearrange("p t j -> p (t j)"),
            )

        def take(window, result, s0, s1):
            nc.vector.tensor_copy(result[:, s0:s1], window[:].indirect(offs_sb[:, s0 // 16 : s1 // 16]))

        cast(0, 0)
        cast(0, 1)
        quantize(0, 0)
        cast(0, 2)
        quantize(0, 1)
        quantize(0, 2)
        take(codes[0], slot_codes[0], *WORD0_PIECES[0])
        take(codes[0], slot_codes[0], *WORD0_PIECES[1])
        cast(1, 0)
        cast(1, 1)
        quantize(1, 0)
        take(codes[0], slot_codes[0], *WORD0_PIECES[2])
        cast(1, 2)
        quantize(1, 1)
        quantize(1, 2)

        def multiply(acc, a, h, e, b0, b1):
            nc.tensor.matmul_mx(
                out=acc[:],
                lhsT=(w8_sb[:, e, 512 * h : 512 * (h + 1)].bitcast(FP8X4), w4_sb[:, e, 256 * h : 256 * (h + 1)].bitcast(FP4X4))[a],
                lhsT_scale=w_scales[4 * (1 - a) :, e, P * h : P * (h + 1)],
                rhs=slot_codes[a][:, b0:b1].bitcast(FP8X4),
                rhs_scale=slot_scales[4 * (1 - a) :, b0:b1],
                start=a == 0,
                stop=a == 1,
            )

        def empty(acc, h, e, b0, b1):
            if h == 0 and b0 == 1920:
                nc.vector.tensor_scalar(y[h][:, b0:b1], acc[:], b_sb[:, h, e : e + 1], 0.0, op0=ADD, op1=MAX)
            else:
                nc.scalar.activation(y[h][:, b0:b1], acc[:], RELU, bias=b_sb[:, h, e : e + 1])

        def experts(h, banks):
            for e, b0, b1 in banks:
                acc = psum.tile([P, b1 - b0], F32, name="acc")
                multiply(acc, 0, h, e, b0, b1)
                multiply(acc, 1, h, e, b0, b1)
                empty(acc, h, e, b0, b1)

        for i, (s0, s1, banks) in enumerate(PIECES[:-1]):
            take(scales, slot_scales, *((0, 896), (896, 1792), (1792, 2560))[i])
            take(codes[1], slot_codes[1], s0, s1)
            experts(0, banks)
            if i == 0:
                experts(1, banks)
        s0, s1, banks = PIECES[-1]
        sums = []
        for e, b0, b1 in banks:
            acc = psum.tile([P, b1 - b0], F32, name="acc")
            sums.append(acc)
            multiply(acc, 0, 0, e, b0, b1)
        take(codes[1], slot_codes[1], s0, s1)
        for acc, (e, b0, b1) in zip(sums, banks):
            multiply(acc, 1, 0, e, b0, b1)
            empty(acc, 0, e, b0, b1)
        for s0, s1, banks in PIECES[1:]:
            experts(1, banks)

        def product(c, i):
            h, t0, t1 = COMBINE[c]
            result = keep.tile([P, t1 - t0], F32, name=f"product{c}_{i}")
            pos = (pos1_sb, pos2_sb)[i]
            nc.vector.tensor_tensor(result[:], y[h][:].indirect(pos[:, t0 // 16 : t1 // 16]), gates[i][:, t0:t1], MULT)
            return result

        def add_and_store(c, first, second):
            h, t0, t1 = COMBINE[c]
            total = keep.tile([P, t1 - t0], F32, name=f"total{c}")
            nc.vector.tensor_tensor(total[:], first[:], second[:], ADD)
            nc.sync.dma_start(out=out[P * h : P * (h + 1), t0:t1], in_=total[:])

        held = None
        for c in range(len(COMBINE)):
            first = product(c, 0)
            if held:
                add_and_store(c - 1, *held)
            held = (first, product(c, 1))
        add_and_store(len(COMBINE) - 1, *held)
